import numpy as np
import ml_dtypes


def mxq(x, axis, fmt="e4m3"):
    dtype, down = {"e4m3": (ml_dtypes.float8_e4m3fn, 7), "e5m2": (ml_dtypes.float8_e5m2, 14)}[fmt]
    v = np.moveaxis(np.asarray(x, np.float32).astype(ml_dtypes.bfloat16).astype(np.float64), axis, -1)
    blocks = v.reshape(v.shape[:-1] + (-1, 32))
    amax = np.abs(blocks).max(-1, keepdims=True)
    byte = np.maximum(np.where(amax > 0, np.frexp(amax)[1] - 1 + 127, 0) - down, 1)
    scale = np.exp2(byte - 127.0)
    codes = (blocks / scale).astype(np.float32).astype(dtype).astype(np.float64)
    return np.moveaxis((codes * scale).reshape(v.shape), -1, axis)


WIDE = False


def mx_kscale(k):
    if not WIDE:
        return np.ones(k)
    levels = np.array([10, -10, 5, -5, 0])
    if k % 512:
        return np.exp2(np.random.permutation(np.resize(levels, k // 32))).repeat(32)
    a = np.empty((k // 512, 16))
    for p in range(k // 512):
        a[p, :8] = np.random.permutation(np.resize(levels, 8))
        for g in range(8):
            far = levels[np.abs(levels - a[p, g]) >= 10]
            a[p, g + 8] = far[np.random.randint(len(far))]
    return np.exp2(a.ravel()).repeat(32)


def f64(x):
    return np.asarray(x).astype(np.float64)


def striped(idx):
    return np.tile(np.asarray(idx).reshape(-1, 16).T, (8, 1)).astype(np.uint16)


def unstriped(offs):
    return offs[:16].T.reshape(-1).astype(np.int64)


E2M1 = np.array([0.0, 0.5, 1.0, 1.5, 2.0, 3.0, 4.0, 6.0, -0.0, -0.5, -1.0, -1.5, -2.0, -3.0, -4.0, -6.0])


def pack_weight(w, fmt):
    k, n = w.shape
    w = f64(np.asarray(w, np.float32).astype(ml_dtypes.bfloat16)).reshape(k // 32, 32, n)
    amax = np.abs(w).max(1)
    if fmt == "e4m3":
        byte = np.frexp(amax)[1] - 1 + 127 - 7
    else:
        mant, ex = np.frexp(amax / 6.0)
        byte = np.where(mant > 0.5, ex, ex - 1) + 127
    byte = np.clip(np.where(amax > 0, byte, 1), 1, 254)
    scaled = (w * np.exp2(127.0 - byte)[:, None, :]).reshape(k, n).astype(np.float32)
    by_word = np.ascontiguousarray(scaled.reshape(k // 512, 128, 4, n).transpose(0, 1, 3, 2))
    if fmt == "e4m3":
        words = by_word.astype(ml_dtypes.float8_e4m3fn).view(np.uint8)
    else:
        c = by_word.astype(ml_dtypes.float4_e2m1fn).view(np.uint8) & 0xF
        words = (c[..., 0::2] | (c[..., 1::2] << 4)).reshape(k // 512, 128, 2 * n)
    return np.ascontiguousarray(words), np.ascontiguousarray(byte.astype(np.uint8).reshape(k // 512, 16, n))


def unpack_weight(words, scales, fmt):
    g, _, n = scales.shape
    words = np.ascontiguousarray(words).reshape(g, 128, n, -1)
    if fmt == "e4m3":
        vals = words.view(ml_dtypes.float8_e4m3fn).astype(np.float64)
    else:
        nib = np.empty((g, 128, n, 4), np.uint8)
        nib[..., 0::2] = words & 0xF
        nib[..., 1::2] = words >> 4
        vals = E2M1[nib]
    vals = vals * np.repeat(np.exp2(scales.astype(np.float64) - 127.0), 8, axis=1)[..., None]
    return vals.transpose(0, 1, 3, 2).reshape(g * 512, n)


def softplus(v):
    return np.log(1.0 + np.exp(v))


D, T, V, I, Q = 512, 2048, 1024, 512, 128


def setup_inputs():
    n = np.random.standard_normal
    idx = np.random.permutation(T)[:V]
    idx2 = np.random.randint(0, V, I)
    idx3 = np.random.randint(0, V, I)
    idx4 = np.random.randint(0, V, I)
    fd = mx_kscale(D)
    nodesp = pack_weight(n((D, T)) / fd[:, None], "e4m3")
    return {
        "hid": (n((D, Q)) * 1.5 / np.sqrt(D) * fd[:, None]).astype(np.float32),
        "nodes_words": nodesp[0],
        "nodes_scales": nodesp[1],
        "s1": (np.random.uniform(-1.5, 1.5, (1, I))).astype(np.float32),
        "s2": (np.random.uniform(-1.5, 1.5, (1, I))).astype(np.float32),
        "s3": (np.random.uniform(-1.5, 1.5, (1, I))).astype(np.float32),
        "offs": striped(idx),
        "offs2": striped(idx2),
        "offs3": striped(idx3),
        "offs4": striped(idx4),
    }


def reference(hid, nodes_words, nodes_scales, s1, s2, s3, offs, offs2, offs3, offs4):
    idx = unstriped(offs)
    idx2 = unstriped(offs2)
    idx3 = unstriped(offs3)
    idx4 = unstriped(offs4)
    nodesu = unpack_weight(nodes_words, nodes_scales, "e4m3")
    hidq = mxq(f64(hid), 0, "e4m3")
    nodesidxg = nodesu[:, idx]
    a = hidq.T @ nodesidxg
    y = (softplus(a[:, idx2] * f64(s1)) + softplus(a[:, idx3] * f64(s2)) + softplus(a[:, idx4] * f64(s3))) * (-1.0)
    return y

@@ -1,0 +1,149 @@
+from contextlib import ExitStack
+
+import concourse.mybir as mybir
+from concourse.masks import make_identity
+
+D, T, V, I, Q = 512, 2048, 1024, 512, 128
+FLOPS = 2 * D * Q * V
+
+F32 = mybir.dt.float32
+BF16 = mybir.dt.bfloat16
+I32 = mybir.dt.int32
+U32 = mybir.dt.uint32
+U16 = mybir.dt.uint16
+U8 = mybir.dt.uint8
+FP8X4 = mybir.dt.float8_e4m3fn_x4
+ALU = mybir.AluOpType
+ACT = mybir.ActivationFunctionType
+
+P = 128
+PACK = 4
+STRIPE = 16
+CAP = 14.0
+
+
+def tile_attend_codepaths_kernel(tc, hid, nodes_words, nodes_scales, s1, s2, s3, offs, offs2, offs3, offs4, out):
+    nc = tc.nc
+    with ExitStack() as ctx:
+        lists = ctx.enter_context(tc.tile_pool(name="lists", bufs=1))
+        keep = ctx.enter_context(tc.tile_pool(name="keep", bufs=1))
+        psum = ctx.enter_context(tc.psum_pool(name="psum", bufs=1))
+
+        node_list = lists.tile([P, V // STRIPE], U16, name="node_list")
+        path_lists = [lists.tile([P, I // STRIPE], U16, name="path_list%d" % k) for k in range(3)]
+
+        store_scales = keep.tile([P, T], U8, name="store_scales", align_bytes=64)
+        cap_seed = keep.tile([P, 1], F32, name="cap_seed", tag="store_words", align_bytes=64)
+        hid_raw = keep.tile([P, PACK, Q], F32, name="hid_raw")
+        ident = keep.tile([P, P], F32, name="ident")
+        minus_cap = keep.tile([P, 1], F32, name="minus_cap")
+        small = keep.tile([P, 4, 8], F32, name="small")
+        plus_cap = small[:, 0, 0:1]
+        floor = keep.tile([P, 1], F32, name="floor")
+
+        nc.vector.memset(store_scales[:].bitcast(I32), 0)
+        nc.vector.memset(cap_seed[:], CAP)
+        nc.vector.tensor_scalar(minus_cap[:], cap_seed[:], -1.0, None, ALU.mult)
+        nc.vector.memset(small[:], CAP)
+        nc.vector.memset(ident[:], 0.0)
+        make_identity(nc, ident[:], nomemset=True)
+        nc.scalar.activation(floor[:], minus_cap[:], ACT.Sigmoid)
+
+        nc.sync.dma_start(node_list[:], offs)
+        for path_list, src in zip(path_lists, (offs2, offs3, offs4)):
+            nc.sync.dma_start(path_list[:], src)
+        nc.sync.dma_start(hid_raw[:], hid.rearrange("(p j) q -> p j q", j=PACK))
+        for quad in range(4):
+            nc.sync.dma_start(
+                store_scales[32 * quad : 32 * quad + 4, :].bitcast(I32),
+                nodes_scales[0][4 * quad : 4 * quad + 4, :].bitcast(I32),
+            )
+        store_words = keep.tile([P, T], U32, name="store_words", tag="store_words", align_bytes=64)
+        nc.sync.dma_start(store_words[:].bitcast(I32), nodes_words[0].rearrange("p n t -> p (n t)").bitcast(I32))
+
+        hid_bf = keep.tile([P, Q, PACK], BF16, name="hid_bf", align_bytes=64)
+        nc.scalar.copy(hid_bf[:], hid_raw[:].rearrange("p j q -> p q j"))
+        hid_words = keep.tile([P, Q], U32, name="hid_words", align_bytes=64)
+        hid_scales = keep.tile([P, Q], U8, name="hid_scales", align_bytes=64)
+        nc.vector.quantize_mx(
+            out=hid_words[:].bitcast(FP8X4), scales=hid_scales[:], in_=hid_bf[:].rearrange("p q j -> p (q j)")
+        )
+
+        minus_s = []
+        for k, src in enumerate((s1, s2, s3)):
+            cols = small[:, k + 1, 0:PACK]
+            nc.scalar.dma_start(cols, src.rearrange("o (p c) -> (o p) c", c=PACK))
+            bank = psum.tile([P, PACK, P], F32, name="s_bank%d" % k)
+            for c in range(PACK):
+                nc.tensor.transpose(bank[:, c, :], cols[:, c : c + 1].to_broadcast([P, P]), ident[:])
+            row = keep.tile([P, I], F32, name="minus_s%d" % k)
+            nc.scalar.mul(row[:].rearrange("q (p c) -> q p c", c=PACK), bank[:].rearrange("q c p -> q p c"), -1.0)
+            minus_s.append(row)
+
+        node_scales = keep.tile([P, V], U8, name="node_scales", align_bytes=64)
+        nc.vector.tensor_copy(node_scales[:], store_scales[:].indirect(node_list[:]))
+
+        scores = keep.tile([P, V], F32, name="scores")
+        pieces = ((0, 512, (512,)), (512, 256, (256,)), (768, 256, (128, 128)))
+        for first, width, passes in pieces:
+            node_words = keep.tile([P, width], U32, name="node_words%d" % first, align_bytes=64)
+            nc.vector.tensor_copy(
+                node_words[:], store_words[:].indirect(node_list[:, first // STRIPE : (first + width) // STRIPE])
+            )
+            at = 0
+            for n in passes:
+                bank = psum.tile([P, n], F32, name="score_bank%d" % (first + at))
+                nc.tensor.matmul_mx(
+                    out=bank[:],
+                    lhsT=hid_words[:].bitcast(FP8X4),
+                    lhsT_scale=hid_scales[:],
+                    rhs=node_words[:, at : at + n].bitcast(FP8X4),
+                    rhs_scale=node_scales[:, first + at : first + at + n],
+                    start=True,
+                    stop=True,
+                )
+                cols = slice(first + at, first + at + n)
+                if first + at + n == V:
+                    nc.vector.tensor_copy(scores[:, cols], bank[:])
+                else:
+                    nc.scalar.copy(scores[:, cols], bank[:])
+                at += n
+
+        y = [keep.tile([P, I], F32, name="y%d" % k) for k in range(3)]
+        p = [keep.tile([P, I], F32, name="p%d" % k) for k in range(3)]
+        nc.vector.tensor_tensor(y[0][:], scores[:].indirect(path_lists[0][:]), minus_s[0][:], ALU.mult)
+        raised = keep.tile([P, I], F32, name="raised")
+        excess0 = keep.tile([P, I], F32, name="excess0")
+        nc.scalar.activation(raised[:], y[0][:], ACT.Relu, bias=plus_cap)
+        nc.scalar.activation(p[0][:], raised[:], ACT.Sigmoid, bias=minus_cap[:])
+        nc.scalar.activation(excess0[:], y[0][:], ACT.Relu, bias=minus_cap[:], scale=-1.0)
+
+        nc.vector.tensor_tensor(y[1][:], scores[:].indirect(path_lists[1][:]), minus_s[1][:], ALU.mult)
+        nc.scalar.activation(p[1][:], y[1][:], ACT.Sigmoid)
+
+        for first, width in ((0, 384), (384, 128)):
+            cols = slice(first, first + width)
+            nc.vector.tensor_tensor(
+                y[2][:, cols],
+                scores[:].indirect(path_lists[2][:, first // STRIPE : (first + width) // STRIPE]),
+                minus_s[2][:, cols],
+                ALU.mult,
+            )
+            nc.scalar.activation(p[2][:, cols], y[2][:, cols], ACT.Sigmoid)
+
+        prod01 = keep.tile([P, I], F32, name="prod01")
+        prod = keep.tile([P, I], F32, name="prod")
+        low01 = keep.tile([P, I], F32, name="low01")
+        low = keep.tile([P, I], F32, name="low")
+        nc.vector.scalar_tensor_tensor(prod01[:], p[1][:], floor[:], p[0][:], ALU.max, ALU.mult)
+        nc.vector.scalar_tensor_tensor(low01[:], y[1][:], -CAP, excess0[:], ALU.min, ALU.subtract)
+        nc.vector.scalar_tensor_tensor(prod[:], p[2][:], floor[:], prod01[:], ALU.max, ALU.mult)
+        nc.vector.scalar_tensor_tensor(low[:], y[2][:], -CAP, low01[:], ALU.min, ALU.add)
+
+        for half in range(2):
+            cols = slice(half * I // 2, (half + 1) * I // 2)
+            logp = keep.tile([P, I // 2], F32, name="logp%d" % half)
+            nc.scalar.activation(logp[:], prod[:, cols], ACT.Ln)
+            result = keep.tile([P, I // 2], F32, name="result%d" % half)
+            nc.vector.scalar_tensor_tensor(result[:], low[:, cols], 2 * CAP, logp[:], ALU.add, ALU.add)
+            nc.sync.dma_start(out[:, cols], result[:])

@@ -20,6 +20,7 @@ P = 128
 PACK = 4
 STRIPE = 16
 CAP = 14.0
+ROW0 = P - 16
 
 
 def tile_attend_codepaths_kernel(tc, hid, nodes_words, nodes_scales, s1, s2, s3, offs, offs2, offs3, offs4, out):
@@ -33,33 +34,31 @@ def tile_attend_codepaths_kernel(tc, hid, nodes_words, nodes_scales, s1, s2, s3,
         path_lists = [lists.tile([P, I // STRIPE], U16, name="path_list%d" % k) for k in range(3)]
 
         store_scales = keep.tile([P, T], U8, name="store_scales", align_bytes=64)
-        cap_seed = keep.tile([P, 1], F32, name="cap_seed", tag="store_words", align_bytes=64)
+        store_words = keep.tile([P, T], U32, name="store_words", align_bytes=64)
+        node_scales = keep.tile([P, V], U8, name="node_scales", align_bytes=64)
         hid_raw = keep.tile([P, PACK, Q], F32, name="hid_raw")
         ident = keep.tile([P, P], F32, name="ident")
         minus_cap = keep.tile([P, 1], F32, name="minus_cap")
-        small = keep.tile([P, 4, 8], F32, name="small")
-        plus_cap = small[:, 0, 0:1]
+        plus_cap = keep.tile([P, 1], F32, name="plus_cap")
         floor = keep.tile([P, 1], F32, name="floor")
 
-        nc.vector.memset(store_scales[:].bitcast(I32), 0)
-        nc.vector.memset(cap_seed[:], CAP)
-        nc.vector.tensor_scalar(minus_cap[:], cap_seed[:], -1.0, None, ALU.mult)
-        nc.vector.memset(small[:], CAP)
+        nc.sync.dma_start(node_list[:], offs)
+        nc.sync.dma_start(store_scales[ROW0:P, :].bitcast(I32), nodes_scales[0].bitcast(I32))
+        for path_list, src in zip(path_lists, (offs2, offs3, offs4)):
+            nc.sync.dma_start(path_list[:], src)
+        s_cols = [keep.tile([P, PACK], F32, name="s_cols%d" % k) for k in range(3)]
+        for cols, src, queue in zip(s_cols, (s1, s2, s3), (nc.sync, nc.gpsimd, nc.gpsimd)):
+            queue.dma_start(cols[:], src.rearrange("o (p c) -> (o p) c", c=PACK))
+        nc.sync.dma_start(store_words[:].bitcast(I32), nodes_words[0].rearrange("p n t -> p (n t)").bitcast(I32))
+        nc.sync.dma_start(hid_raw[:], hid.rearrange("(p j) q -> p j q", j=PACK))
+
+        nc.vector.memset(minus_cap[:], -CAP)
+        nc.vector.memset(store_scales[0:ROW0, :].bitcast(I32), 0)
+        nc.vector.memset(node_scales[:].bitcast(I32), 0)
+        nc.vector.memset(plus_cap[:], CAP)
         nc.vector.memset(ident[:], 0.0)
         make_identity(nc, ident[:], nomemset=True)
         nc.scalar.activation(floor[:], minus_cap[:], ACT.Sigmoid)
-
-        nc.sync.dma_start(node_list[:], offs)
-        for path_list, src in zip(path_lists, (offs2, offs3, offs4)):
-            nc.sync.dma_start(path_list[:], src)
-        nc.sync.dma_start(hid_raw[:], hid.rearrange("(p j) q -> p j q", j=PACK))
-        for quad in range(4):
-            nc.sync.dma_start(
-                store_scales[32 * quad : 32 * quad + 4, :].bitcast(I32),
-                nodes_scales[0][4 * quad : 4 * quad + 4, :].bitcast(I32),
-            )
-        store_words = keep.tile([P, T], U32, name="store_words", tag="store_words", align_bytes=64)
-        nc.sync.dma_start(store_words[:].bitcast(I32), nodes_words[0].rearrange("p n t -> p (n t)").bitcast(I32))
 
         hid_bf = keep.tile([P, Q, PACK], BF16, name="hid_bf", align_bytes=64)
         nc.scalar.copy(hid_bf[:], hid_raw[:].rearrange("p j q -> p q j"))
@@ -69,19 +68,29 @@ def tile_attend_codepaths_kernel(tc, hid, nodes_words, nodes_scales, s1, s2, s3,
             out=hid_words[:].bitcast(FP8X4), scales=hid_scales[:], in_=hid_bf[:].rearrange("p q j -> p (q j)")
         )
 
-        minus_s = []
-        for k, src in enumerate((s1, s2, s3)):
-            cols = small[:, k + 1, 0:PACK]
-            nc.scalar.dma_start(cols, src.rearrange("o (p c) -> (o p) c", c=PACK))
-            bank = psum.tile([P, PACK, P], F32, name="s_bank%d" % k)
+        def spread(k):
+            bank = psum.tile([P, PACK, P], F32, name="s_bank%d" % k, tag="bank%d" % k)
             for c in range(PACK):
-                nc.tensor.transpose(bank[:, c, :], cols[:, c : c + 1].to_broadcast([P, P]), ident[:])
+                nc.tensor.transpose(bank[:, c, :], s_cols[k][:, c : c + 1].to_broadcast([P, P]), ident[:])
             row = keep.tile([P, I], F32, name="minus_s%d" % k)
-            nc.scalar.mul(row[:].rearrange("q (p c) -> q p c", c=PACK), bank[:].rearrange("q c p -> q p c"), -1.0)
-            minus_s.append(row)
+            dst = row[:].rearrange("q (p c) -> q p c", c=PACK)
+            src = bank[:].rearrange("q c p -> q p c")
+            nc.scalar.mul(dst, src, -1.0)
+            return row
 
-        node_scales = keep.tile([P, V], U8, name="node_scales", align_bytes=64)
-        nc.vector.tensor_copy(node_scales[:], store_scales[:].indirect(node_list[:]))
+        minus_s = [spread(k) for k in range(3)]
+
+        for half in range(2):
+            picked = keep.tile([P, V // 2], U8, name="picked%d" % half, align_bytes=64)
+            first = half * V // 2
+            nc.vector.tensor_copy(
+                picked[:], store_scales[:].indirect(node_list[:, first // STRIPE : (first + V // 2) // STRIPE])
+            )
+            for quad in range(4):
+                nc.sync.dma_start(
+                    node_scales[32 * quad : 32 * quad + 4, first : first + V // 2].bitcast(I32),
+                    picked[ROW0 + 4 * quad : ROW0 + 4 * quad + 4, :].bitcast(I32),
+                )
 
         scores = keep.tile([P, V], F32, name="scores")
         pieces = ((0, 512, (512,)), (512, 256, (256,)), (768, 256, (128, 128)))
@@ -92,7 +101,7 @@ def tile_attend_codepaths_kernel(tc, hid, nodes_words, nodes_scales, s1, s2, s3,
             )
             at = 0
             for n in passes:
-                bank = psum.tile([P, n], F32, name="score_bank%d" % (first + at))
+                bank = psum.tile([P, n], F32, name="score_bank%d" % (first + at), tag="bank2" if first == 0 else "score%d" % (first + at))
                 nc.tensor.matmul_mx(
                     out=bank[:],
                     lhsT=hid_words[:].bitcast(FP8X4),
@@ -103,7 +112,7 @@ def tile_attend_codepaths_kernel(tc, hid, nodes_words, nodes_scales, s1, s2, s3,
                     stop=True,
                 )
                 cols = slice(first + at, first + at + n)
-                if first + at + n == V:
+                if first + width == V:
                     nc.vector.tensor_copy(scores[:, cols], bank[:])
                 else:
                     nc.scalar.copy(scores[:, cols], bank[:])
@@ -111,11 +120,18 @@ def tile_attend_codepaths_kernel(tc, hid, nodes_words, nodes_scales, s1, s2, s3,
 
         y = [keep.tile([P, I], F32, name="y%d" % k) for k in range(3)]
         p = [keep.tile([P, I], F32, name="p%d" % k) for k in range(3)]
-        nc.vector.tensor_tensor(y[0][:], scores[:].indirect(path_lists[0][:]), minus_s[0][:], ALU.mult)
         raised = keep.tile([P, I], F32, name="raised")
         excess0 = keep.tile([P, I], F32, name="excess0")
-        nc.scalar.activation(raised[:], y[0][:], ACT.Relu, bias=plus_cap)
-        nc.scalar.activation(p[0][:], raised[:], ACT.Sigmoid, bias=minus_cap[:])
+        for first, width in ((0, 256), (256, 256)):
+            cols = slice(first, first + width)
+            nc.vector.tensor_tensor(
+                y[0][:, cols],
+                scores[:].indirect(path_lists[0][:, first // STRIPE : (first + width) // STRIPE]),
+                minus_s[0][:, cols],
+                ALU.mult,
+            )
+            nc.scalar.activation(raised[:, cols], y[0][:, cols], ACT.Relu, bias=plus_cap[:])
+            nc.scalar.activation(p[0][:, cols], raised[:, cols], ACT.Sigmoid, bias=minus_cap[:])
         nc.scalar.activation(excess0[:], y[0][:], ACT.Relu, bias=minus_cap[:], scale=-1.0)
 
         nc.vector.tensor_tensor(y[1][:], scores[:].indirect(path_lists[1][:]), minus_s[1][:], ALU.mult)
@@ -140,10 +156,10 @@ def tile_attend_codepaths_kernel(tc, hid, nodes_words, nodes_scales, s1, s2, s3,
         nc.vector.scalar_tensor_tensor(prod[:], p[2][:], floor[:], prod01[:], ALU.max, ALU.mult)
         nc.vector.scalar_tensor_tensor(low[:], y[2][:], -CAP, low01[:], ALU.min, ALU.add)
 
-        for half in range(2):
-            cols = slice(half * I // 2, (half + 1) * I // 2)
-            logp = keep.tile([P, I // 2], F32, name="logp%d" % half)
+        result = keep.tile([P, I], F32, name="result")
+        for first, width in ((0, 128), (128, 256), (384, 128)):
+            cols = slice(first, first + width)
+            logp = keep.tile([P, width], F32, name="logp%d" % first)
             nc.scalar.activation(logp[:], prod[:, cols], ACT.Ln)
-            result = keep.tile([P, I // 2], F32, name="result%d" % half)
-            nc.vector.scalar_tensor_tensor(result[:], low[:, cols], 2 * CAP, logp[:], ALU.add, ALU.add)
-            nc.sync.dma_start(out[:, cols], result[:])
+            nc.vector.scalar_tensor_tensor(result[:, cols], low[:, cols], 2 * CAP, logp[:], ALU.add, ALU.add)
+            nc.sync.dma_start(out[:, cols], result[:, cols])

@@ -39,26 +39,29 @@ def tile_attend_codepaths_kernel(tc, hid, nodes_words, nodes_scales, s1, s2, s3,
         hid_raw = keep.tile([P, PACK, Q], F32, name="hid_raw")
         ident = keep.tile([P, P], F32, name="ident")
         minus_cap = keep.tile([P, 1], F32, name="minus_cap")
-        plus_cap = keep.tile([P, 1], F32, name="plus_cap")
+        small = keep.tile([P, 3, 8], F32, name="small")
+        plus_cap = small[:, 0, 0:1]
         floor = keep.tile([P, 1], F32, name="floor")
 
         nc.sync.dma_start(node_list[:], offs)
         nc.sync.dma_start(store_scales[ROW0:P, :].bitcast(I32), nodes_scales[0].bitcast(I32))
         for path_list, src in zip(path_lists, (offs2, offs3, offs4)):
             nc.sync.dma_start(path_list[:], src)
-        s_cols = [keep.tile([P, PACK], F32, name="s_cols%d" % k) for k in range(3)]
-        for cols, src, queue in zip(s_cols, (s1, s2, s3), (nc.sync, nc.gpsimd, nc.gpsimd)):
-            queue.dma_start(cols[:], src.rearrange("o (p c) -> (o p) c", c=PACK))
-        nc.sync.dma_start(store_words[:].bitcast(I32), nodes_words[0].rearrange("p n t -> p (n t)").bitcast(I32))
         nc.sync.dma_start(hid_raw[:], hid.rearrange("(p j) q -> p j q", j=PACK))
+        first_cols = keep.tile([P, PACK], F32, name="first_cols")
+        s_cols = [first_cols[:], small[:, 1, 0:PACK], small[:, 2, 0:PACK]]
+        nc.sync.dma_start(s_cols[0], s1.rearrange("o (p c) -> (o p) c", c=PACK))
+        nc.sync.dma_start(store_words[:].bitcast(I32), nodes_words[0].rearrange("p n t -> p (n t)").bitcast(I32))
 
         nc.vector.memset(minus_cap[:], -CAP)
         nc.vector.memset(store_scales[0:ROW0, :].bitcast(I32), 0)
         nc.vector.memset(node_scales[:].bitcast(I32), 0)
-        nc.vector.memset(plus_cap[:], CAP)
+        nc.vector.memset(small[:], CAP)
         nc.vector.memset(ident[:], 0.0)
         make_identity(nc, ident[:], nomemset=True)
         nc.scalar.activation(floor[:], minus_cap[:], ACT.Sigmoid)
+        for cols, src in zip(s_cols[1:], (s2, s3)):
+            nc.scalar.dma_start(cols, src.rearrange("o (p c) -> (o p) c", c=PACK))
 
         hid_bf = keep.tile([P, Q, PACK], BF16, name="hid_bf", align_bytes=64)
         nc.scalar.copy(hid_bf[:], hid_raw[:].rearrange("p j q -> p q j"))
@@ -69,7 +72,7 @@ def tile_attend_codepaths_kernel(tc, hid, nodes_words, nodes_scales, s1, s2, s3,
         )
 
         def spread(k):
-            bank = psum.tile([P, PACK, P], F32, name="s_bank%d" % k, tag="bank%d" % k)
+            bank = psum.tile([P, PACK, P], F32, name="s_bank%d" % k)
             for c in range(PACK):
                 nc.tensor.transpose(bank[:, c, :], s_cols[k][:, c : c + 1].to_broadcast([P, P]), ident[:])
             row = keep.tile([P, I], F32, name="minus_s%d" % k)
@@ -101,7 +104,7 @@ def tile_attend_codepaths_kernel(tc, hid, nodes_words, nodes_scales, s1, s2, s3,
             )
             at = 0
             for n in passes:
-                bank = psum.tile([P, n], F32, name="score_bank%d" % (first + at), tag="bank2" if first == 0 else "score%d" % (first + at))
+                bank = psum.tile([P, n], F32, name="score_bank%d" % (first + at))
                 nc.tensor.matmul_mx(
                     out=bank[:],
                     lhsT=hid_words[:].bitcast(FP8X4),
@@ -130,7 +133,7 @@ def tile_attend_codepaths_kernel(tc, hid, nodes_words, nodes_scales, s1, s2, s3,
                 minus_s[0][:, cols],
                 ALU.mult,
             )
-            nc.scalar.activation(raised[:, cols], y[0][:, cols], ACT.Relu, bias=plus_cap[:])
+            nc.scalar.activation(raised[:, cols], y[0][:, cols], ACT.Relu, bias=plus_cap)
             nc.scalar.activation(p[0][:, cols], raised[:, cols], ACT.Sigmoid, bias=minus_cap[:])
         nc.scalar.activation(excess0[:], y[0][:], ACT.Relu, bias=minus_cap[:], scale=-1.0)
 

@@ -44,14 +44,15 @@ def tile_attend_codepaths_kernel(tc, hid, nodes_words, nodes_scales, s1, s2, s3,
         floor = keep.tile([P, 1], F32, name="floor")
 
         nc.sync.dma_start(node_list[:], offs)
-        nc.sync.dma_start(store_scales[ROW0:P, :].bitcast(I32), nodes_scales[0].bitcast(I32))
-        for path_list, src in zip(path_lists, (offs2, offs3, offs4)):
+        nc.scalar.dma_start(store_scales[ROW0:P, :].bitcast(I32), nodes_scales[0].bitcast(I32))
+        for path_list, src in zip(path_lists[:2], (offs2, offs3)):
             nc.sync.dma_start(path_list[:], src)
-        nc.sync.dma_start(hid_raw[:], hid.rearrange("(p j) q -> p j q", j=PACK))
+        nc.scalar.dma_start(hid_raw[:], hid.rearrange("(p j) q -> p j q", j=PACK))
         first_cols = keep.tile([P, PACK], F32, name="first_cols")
         s_cols = [first_cols[:], small[:, 1, 0:PACK], small[:, 2, 0:PACK]]
-        nc.sync.dma_start(s_cols[0], s1.rearrange("o (p c) -> (o p) c", c=PACK))
+        nc.scalar.dma_start(s_cols[0], s1.rearrange("o (p c) -> (o p) c", c=PACK))
         nc.sync.dma_start(store_words[:].bitcast(I32), nodes_words[0].rearrange("p n t -> p (n t)").bitcast(I32))
+        nc.sync.dma_start(path_lists[2][:], offs4)
 
         nc.vector.memset(minus_cap[:], -CAP)
         nc.vector.memset(store_scales[0:ROW0, :].bitcast(I32), 0)
@@ -83,15 +84,14 @@ def tile_attend_codepaths_kernel(tc, hid, nodes_words, nodes_scales, s1, s2, s3,
 
         minus_s = [spread(k) for k in range(3)]
 
-        for half in range(2):
-            picked = keep.tile([P, V // 2], U8, name="picked%d" % half, align_bytes=64)
-            first = half * V // 2
+        for first, width in ((0, 768), (768, 256)):
+            picked = keep.tile([P, width], U8, name="picked%d" % first, align_bytes=64)
             nc.vector.tensor_copy(
-                picked[:], store_scales[:].indirect(node_list[:, first // STRIPE : (first + V // 2) // STRIPE])
+                picked[:], store_scales[:].indirect(node_list[:, first // STRIPE : (first + width) // STRIPE])
             )
             for quad in range(4):
                 nc.sync.dma_start(
-                    node_scales[32 * quad : 32 * quad + 4, first : first + V // 2].bitcast(I32),
+                    node_scales[32 * quad : 32 * quad + 4, first : first + width].bitcast(I32),
                     picked[ROW0 + 4 * quad : ROW0 + 4 * quad + 4, :].bitcast(I32),
                 )
 
@@ -115,7 +115,7 @@ def tile_attend_codepaths_kernel(tc, hid, nodes_words, nodes_scales, s1, s2, s3,
                     stop=True,
                 )
                 cols = slice(first + at, first + at + n)
-                if first + width == V:
+                if first + at in (512, 896):
                     nc.vector.tensor_copy(scores[:, cols], bank[:])
                 else:
                     nc.scalar.copy(scores[:, cols], bank[:])
@@ -165,4 +165,4 @@ def tile_attend_codepaths_kernel(tc, hid, nodes_words, nodes_scales, s1, s2, s3,
             logp = keep.tile([P, width], F32, name="logp%d" % first)
             nc.scalar.activation(logp[:], prod[:, cols], ACT.Ln)
             nc.vector.scalar_tensor_tensor(result[:, cols], low[:, cols], 2 * CAP, logp[:], ALU.add, ALU.add)
-            nc.sync.dma_start(out[:, cols], result[:, cols])
+            (nc.scalar if first == 128 else nc.sync).dma_start(out[:, cols], result[:, cols])

@@ -18,151 +18,153 @@ ACT = mybir.ActivationFunctionType
 
 P = 128
 PACK = 4
+QUADRANTS, QUADRANT_ROWS = 4, 32
+BLOCKS = D // 32
 STRIPE = 16
+TERMS = 3
+S_COLS = I // P
 CAP = 14.0
-ROW0 = P - 16
+STAGED = P - BLOCKS
+
+SCALE_PARTS = ((0, 768), (768, 256))
+WORD_PARTS = ((0, ((512, "scalar"),)), (512, ((256, "vector"),)), (768, ((128, "scalar"), (128, "vector"))))
+LOOKUP_PARTS = (((0, 256), (256, 256)), ((0, 512),), ((0, 384), (384, 128)))
+RESULT_PARTS = ((0, 128, "sync"), (128, 256, "scalar"), (384, 128, "sync"))
+
+
+def entries(list_tile, first, count):
+    return list_tile[:, first // STRIPE : (first + count) // STRIPE]
 
 
 def tile_attend_codepaths_kernel(tc, hid, nodes_words, nodes_scales, s1, s2, s3, offs, offs2, offs3, offs4, out):
     nc = tc.nc
+    queues = {"sync": nc.sync, "scalar": nc.scalar}
+    copies = {"scalar": nc.scalar.copy, "vector": nc.vector.tensor_copy}
+
     with ExitStack() as ctx:
         lists = ctx.enter_context(tc.tile_pool(name="lists", bufs=1))
         keep = ctx.enter_context(tc.tile_pool(name="keep", bufs=1))
         psum = ctx.enter_context(tc.psum_pool(name="psum", bufs=1))
 
         node_list = lists.tile([P, V // STRIPE], U16, name="node_list")
-        path_lists = [lists.tile([P, I // STRIPE], U16, name="path_list%d" % k) for k in range(3)]
+        path_lists = [lists.tile([P, I // STRIPE], U16, name="path_list%d" % k) for k in range(TERMS)]
 
         store_scales = keep.tile([P, T], U8, name="store_scales", align_bytes=64)
         store_words = keep.tile([P, T], U32, name="store_words", align_bytes=64)
         node_scales = keep.tile([P, V], U8, name="node_scales", align_bytes=64)
-        hid_raw = keep.tile([P, PACK, Q], F32, name="hid_raw")
+        hid_raw = keep.tile([P, PACK, Q], F32, name="hid_raw", tag="hid_raw")
         ident = keep.tile([P, P], F32, name="ident")
         minus_cap = keep.tile([P, 1], F32, name="minus_cap")
-        small = keep.tile([P, 3, 8], F32, name="small")
-        plus_cap = small[:, 0, 0:1]
+        plus_cap = keep.tile([P, 1], F32, name="plus_cap")
         floor = keep.tile([P, 1], F32, name="floor")
 
+        def load_weights(cols, s):
+            nc.scalar.dma_start(cols[:], s.rearrange("o (p c) -> (o p) c", c=S_COLS))
+
+        s_cols = [keep.tile([P, S_COLS], F32, name="s_cols%d" % k) for k in range(TERMS - 1)]
         nc.sync.dma_start(node_list[:], offs)
-        nc.scalar.dma_start(store_scales[ROW0:P, :].bitcast(I32), nodes_scales[0].bitcast(I32))
+        for cols, s in zip(s_cols, (s1, s2)):
+            load_weights(cols, s)
+        nc.sync.dma_start(store_scales[STAGED:P, :].bitcast(I32), nodes_scales[0].bitcast(I32))
+        nc.sync.dma_start(hid_raw[:], hid.rearrange("(p j) q -> p j q", j=PACK))
         for path_list, src in zip(path_lists[:2], (offs2, offs3)):
             nc.sync.dma_start(path_list[:], src)
-        nc.scalar.dma_start(hid_raw[:], hid.rearrange("(p j) q -> p j q", j=PACK))
-        first_cols = keep.tile([P, PACK], F32, name="first_cols")
-        s_cols = [first_cols[:], small[:, 1, 0:PACK], small[:, 2, 0:PACK]]
-        nc.scalar.dma_start(s_cols[0], s1.rearrange("o (p c) -> (o p) c", c=PACK))
         nc.sync.dma_start(store_words[:].bitcast(I32), nodes_words[0].rearrange("p n t -> p (n t)").bitcast(I32))
         nc.sync.dma_start(path_lists[2][:], offs4)
 
         nc.vector.memset(minus_cap[:], -CAP)
-        nc.vector.memset(store_scales[0:ROW0, :].bitcast(I32), 0)
+        nc.vector.memset(store_scales[0:STAGED, :].bitcast(I32), 0)
         nc.vector.memset(node_scales[:].bitcast(I32), 0)
-        nc.vector.memset(small[:], CAP)
+        nc.vector.memset(plus_cap[:], CAP)
         nc.vector.memset(ident[:], 0.0)
         make_identity(nc, ident[:], nomemset=True)
         nc.scalar.activation(floor[:], minus_cap[:], ACT.Sigmoid)
-        for cols, src in zip(s_cols[1:], (s2, s3)):
-            nc.scalar.dma_start(cols, src.rearrange("o (p c) -> (o p) c", c=PACK))
 
         hid_bf = keep.tile([P, Q, PACK], BF16, name="hid_bf", align_bytes=64)
         nc.scalar.copy(hid_bf[:], hid_raw[:].rearrange("p j q -> p q j"))
+        last_cols = keep.tile([P, S_COLS], F32, name="last_cols", tag="hid_raw")
+        load_weights(last_cols, s3)
+        s_cols.append(last_cols)
         hid_words = keep.tile([P, Q], U32, name="hid_words", align_bytes=64)
         hid_scales = keep.tile([P, Q], U8, name="hid_scales", align_bytes=64)
         nc.vector.quantize_mx(
             out=hid_words[:].bitcast(FP8X4), scales=hid_scales[:], in_=hid_bf[:].rearrange("p q j -> p (q j)")
         )
 
-        def spread(k):
-            bank = psum.tile([P, PACK, P], F32, name="s_bank%d" % k)
-            for c in range(PACK):
-                nc.tensor.transpose(bank[:, c, :], s_cols[k][:, c : c + 1].to_broadcast([P, P]), ident[:])
+        minus_s = []
+        for k in range(TERMS):
+            s_bank = psum.tile([P, S_COLS, P], F32, name="s_bank%d" % k)
+            for c in range(S_COLS):
+                nc.tensor.transpose(s_bank[:, c, :], s_cols[k][:, c : c + 1].to_broadcast([P, P]), ident[:])
             row = keep.tile([P, I], F32, name="minus_s%d" % k)
-            dst = row[:].rearrange("q (p c) -> q p c", c=PACK)
-            src = bank[:].rearrange("q c p -> q p c")
-            nc.scalar.mul(dst, src, -1.0)
-            return row
+            nc.scalar.mul(row[:].rearrange("q (p c) -> q p c", c=S_COLS), s_bank[:].rearrange("q c p -> q p c"), -1.0)
+            minus_s.append(row)
 
-        minus_s = [spread(k) for k in range(3)]
-
-        for first, width in ((0, 768), (768, 256)):
-            picked = keep.tile([P, width], U8, name="picked%d" % first, align_bytes=64)
-            nc.vector.tensor_copy(
-                picked[:], store_scales[:].indirect(node_list[:, first // STRIPE : (first + width) // STRIPE])
-            )
-            for quad in range(4):
+        for first, count in SCALE_PARTS:
+            picked = keep.tile([P, count], U8, name="picked%d" % first, align_bytes=64)
+            nc.vector.tensor_copy(picked[:], store_scales[:].indirect(entries(node_list, first, count)))
+            rows = BLOCKS // QUADRANTS
+            for quad in range(QUADRANTS):
                 nc.sync.dma_start(
-                    node_scales[32 * quad : 32 * quad + 4, first : first + width].bitcast(I32),
-                    picked[ROW0 + 4 * quad : ROW0 + 4 * quad + 4, :].bitcast(I32),
+                    node_scales[QUADRANT_ROWS * quad : QUADRANT_ROWS * quad + rows, first : first + count].bitcast(I32),
+                    picked[STAGED + rows * quad : STAGED + rows * (quad + 1), :].bitcast(I32),
                 )
 
         scores = keep.tile([P, V], F32, name="scores")
-        pieces = ((0, 512, (512,)), (512, 256, (256,)), (768, 256, (128, 128)))
-        for first, width, passes in pieces:
-            node_words = keep.tile([P, width], U32, name="node_words%d" % first, align_bytes=64)
-            nc.vector.tensor_copy(
-                node_words[:], store_words[:].indirect(node_list[:, first // STRIPE : (first + width) // STRIPE])
-            )
+        for first, passes in WORD_PARTS:
+            count = sum(n for n, engine in passes)
+            node_words = keep.tile([P, count], U32, name="node_words%d" % first, align_bytes=64)
+            nc.vector.tensor_copy(node_words[:], store_words[:].indirect(entries(node_list, first, count)))
             at = 0
-            for n in passes:
-                bank = psum.tile([P, n], F32, name="score_bank%d" % (first + at))
+            for n, engine in passes:
+                nodes = slice(first + at, first + at + n)
+                score_bank = psum.tile([P, n], F32, name="score_bank%d" % nodes.start)
                 nc.tensor.matmul_mx(
-                    out=bank[:],
+                    out=score_bank[:],
                     lhsT=hid_words[:].bitcast(FP8X4),
                     lhsT_scale=hid_scales[:],
                     rhs=node_words[:, at : at + n].bitcast(FP8X4),
-                    rhs_scale=node_scales[:, first + at : first + at + n],
+                    rhs_scale=node_scales[:, nodes],
                     start=True,
                     stop=True,
                 )
-                cols = slice(first + at, first + at + n)
-                if first + at in (512, 896):
-                    nc.vector.tensor_copy(scores[:, cols], bank[:])
-                else:
-                    nc.scalar.copy(scores[:, cols], bank[:])
+                copies[engine](scores[:, nodes], score_bank[:])
                 at += n
 
-        y = [keep.tile([P, I], F32, name="y%d" % k) for k in range(3)]
-        p = [keep.tile([P, I], F32, name="p%d" % k) for k in range(3)]
-        raised = keep.tile([P, I], F32, name="raised")
-        excess0 = keep.tile([P, I], F32, name="excess0")
-        for first, width in ((0, 256), (256, 256)):
-            cols = slice(first, first + width)
-            nc.vector.tensor_tensor(
-                y[0][:, cols],
-                scores[:].indirect(path_lists[0][:, first // STRIPE : (first + width) // STRIPE]),
-                minus_s[0][:, cols],
-                ALU.mult,
-            )
-            nc.scalar.activation(raised[:, cols], y[0][:, cols], ACT.Relu, bias=plus_cap)
-            nc.scalar.activation(p[0][:, cols], raised[:, cols], ACT.Sigmoid, bias=minus_cap[:])
-        nc.scalar.activation(excess0[:], y[0][:], ACT.Relu, bias=minus_cap[:], scale=-1.0)
+        y = [keep.tile([P, I], F32, name="y%d" % k) for k in range(TERMS)]
+        chance = [keep.tile([P, I], F32, name="chance%d" % k) for k in range(TERMS)]
+        raised0 = keep.tile([P, I], F32, name="raised0")
+        removed0 = keep.tile([P, I], F32, name="removed0")
 
-        nc.vector.tensor_tensor(y[1][:], scores[:].indirect(path_lists[1][:]), minus_s[1][:], ALU.mult)
-        nc.scalar.activation(p[1][:], y[1][:], ACT.Sigmoid)
+        def look_up(k, first, count):
+            cols = slice(first, first + count)
+            picked_scores = scores[:].indirect(entries(path_lists[k], first, count))
+            nc.vector.tensor_tensor(y[k][:, cols], picked_scores, minus_s[k][:, cols], ALU.mult)
+            return cols
 
-        for first, width in ((0, 384), (384, 128)):
-            cols = slice(first, first + width)
-            nc.vector.tensor_tensor(
-                y[2][:, cols],
-                scores[:].indirect(path_lists[2][:, first // STRIPE : (first + width) // STRIPE]),
-                minus_s[2][:, cols],
-                ALU.mult,
-            )
-            nc.scalar.activation(p[2][:, cols], y[2][:, cols], ACT.Sigmoid)
+        for first, count in LOOKUP_PARTS[0]:
+            cols = look_up(0, first, count)
+            nc.scalar.activation(raised0[:, cols], y[0][:, cols], ACT.Relu, bias=plus_cap[:])
+            nc.scalar.activation(chance[0][:, cols], raised0[:, cols], ACT.Sigmoid, bias=minus_cap[:])
+        nc.scalar.activation(removed0[:], y[0][:], ACT.Relu, bias=minus_cap[:], scale=-1.0)
+        for k in range(1, TERMS):
+            for first, count in LOOKUP_PARTS[k]:
+                cols = look_up(k, first, count)
+                nc.scalar.activation(chance[k][:, cols], y[k][:, cols], ACT.Sigmoid)
 
-        prod01 = keep.tile([P, I], F32, name="prod01")
-        prod = keep.tile([P, I], F32, name="prod")
-        low01 = keep.tile([P, I], F32, name="low01")
-        low = keep.tile([P, I], F32, name="low")
-        nc.vector.scalar_tensor_tensor(prod01[:], p[1][:], floor[:], p[0][:], ALU.max, ALU.mult)
-        nc.vector.scalar_tensor_tensor(low01[:], y[1][:], -CAP, excess0[:], ALU.min, ALU.subtract)
-        nc.vector.scalar_tensor_tensor(prod[:], p[2][:], floor[:], prod01[:], ALU.max, ALU.mult)
-        nc.vector.scalar_tensor_tensor(low[:], y[2][:], -CAP, low01[:], ALU.min, ALU.add)
+        product01 = keep.tile([P, I], F32, name="product01")
+        product = keep.tile([P, I], F32, name="product")
+        below01 = keep.tile([P, I], F32, name="below01")
+        below = keep.tile([P, I], F32, name="below")
+        nc.vector.scalar_tensor_tensor(product01[:], chance[1][:], floor[:], chance[0][:], ALU.max, ALU.mult)
+        nc.vector.scalar_tensor_tensor(below01[:], y[1][:], -CAP, removed0[:], ALU.min, ALU.subtract)
+        nc.vector.scalar_tensor_tensor(product[:], chance[2][:], floor[:], product01[:], ALU.max, ALU.mult)
+        nc.vector.scalar_tensor_tensor(below[:], y[2][:], -CAP, below01[:], ALU.min, ALU.add)
 
         result = keep.tile([P, I], F32, name="result")
-        for first, width in ((0, 128), (128, 256), (384, 128)):
-            cols = slice(first, first + width)
-            logp = keep.tile([P, width], F32, name="logp%d" % first)
-            nc.scalar.activation(logp[:], prod[:, cols], ACT.Ln)
-            nc.vector.scalar_tensor_tensor(result[:, cols], low[:, cols], 2 * CAP, logp[:], ALU.add, ALU.add)
-            (nc.scalar if first == 128 else nc.sync).dma_start(out[:, cols], result[:, cols])
+        for first, count, queue in RESULT_PARTS:
+            cols = slice(first, first + count)
+            log_product = keep.tile([P, count], F32, name="log_product%d" % first)
+            nc.scalar.activation(log_product[:], product[:, cols], ACT.Ln)
+            nc.vector.scalar_tensor_tensor(result[:, cols], below[:, cols], 2 * CAP, log_product[:], ALU.add, ALU.add)
+            queues[queue].dma_start(out[:, cols], result[:, cols])

from contextlib import ExitStack

import concourse.mybir as mybir
from concourse.masks import make_identity

D, T, V, I, Q = 512, 2048, 1024, 512, 128
FLOPS = 2 * D * Q * V

F32 = mybir.dt.float32
BF16 = mybir.dt.bfloat16
I32 = mybir.dt.int32
U32 = mybir.dt.uint32
U16 = mybir.dt.uint16
U8 = mybir.dt.uint8
FP8X4 = mybir.dt.float8_e4m3fn_x4
ALU = mybir.AluOpType
ACT = mybir.ActivationFunctionType

P = 128
PACK = 4
QUADRANTS, QUADRANT_ROWS = 4, 32
BLOCKS = D // 32
STRIPE = 16
TERMS = 3
S_COLS = I // P
CAP = 14.0
STAGED = P - BLOCKS

SCALE_PARTS = ((0, 768), (768, 256))
WORD_PARTS = ((0, ((512, "scalar"),)), (512, ((256, "vector"),)), (768, ((128, "scalar"), (128, "vector"))))
LOOKUP_PARTS = (((0, 256), (256, 256)), ((0, 512),), ((0, 384), (384, 128)))
RESULT_PARTS = ((0, 128, "sync"), (128, 256, "scalar"), (384, 128, "sync"))


def entries(list_tile, first, count):
    return list_tile[:, first // STRIPE : (first + count) // STRIPE]


def tile_attend_codepaths_kernel(tc, hid, nodes_words, nodes_scales, s1, s2, s3, offs, offs2, offs3, offs4, out):
    nc = tc.nc
    queues = {"sync": nc.sync, "scalar": nc.scalar}
    copies = {"scalar": nc.scalar.copy, "vector": nc.vector.tensor_copy}

    with ExitStack() as ctx:
        lists = ctx.enter_context(tc.tile_pool(name="lists", bufs=1))
        keep = ctx.enter_context(tc.tile_pool(name="keep", bufs=1))
        psum = ctx.enter_context(tc.psum_pool(name="psum", bufs=1))

        node_list = lists.tile([P, V // STRIPE], U16, name="node_list")
        path_lists = [lists.tile([P, I // STRIPE], U16, name="path_list%d" % k) for k in range(TERMS)]

        store_scales = keep.tile([P, T], U8, name="store_scales", align_bytes=64)
        store_words = keep.tile([P, T], U32, name="store_words", align_bytes=64)
        node_scales = keep.tile([P, V], U8, name="node_scales", align_bytes=64)
        hid_raw = keep.tile([P, PACK, Q], F32, name="hid_raw", tag="hid_raw")
        ident = keep.tile([P, P], F32, name="ident")
        minus_cap = keep.tile([P, 1], F32, name="minus_cap")
        plus_cap = keep.tile([P, 1], F32, name="plus_cap")
        floor = keep.tile([P, 1], F32, name="floor")

        def load_weights(cols, s):
            nc.scalar.dma_start(cols[:], s.rearrange("o (p c) -> (o p) c", c=S_COLS))

        s_cols = [keep.tile([P, S_COLS], F32, name="s_cols%d" % k) for k in range(TERMS - 1)]
        nc.sync.dma_start(node_list[:], offs)
        for cols, s in zip(s_cols, (s1, s2)):
            load_weights(cols, s)
        nc.sync.dma_start(store_scales[STAGED:P, :].bitcast(I32), nodes_scales[0].bitcast(I32))
        nc.sync.dma_start(hid_raw[:], hid.rearrange("(p j) q -> p j q", j=PACK))
        for path_list, src in zip(path_lists[:2], (offs2, offs3)):
            nc.sync.dma_start(path_list[:], src)
        nc.sync.dma_start(store_words[:].bitcast(I32), nodes_words[0].rearrange("p n t -> p (n t)").bitcast(I32))
        nc.sync.dma_start(path_lists[2][:], offs4)

        nc.vector.memset(minus_cap[:], -CAP)
        nc.vector.memset(store_scales[0:STAGED, :].bitcast(I32), 0)
        nc.vector.memset(node_scales[:].bitcast(I32), 0)
        nc.vector.memset(plus_cap[:], CAP)
        nc.vector.memset(ident[:], 0.0)
        make_identity(nc, ident[:], nomemset=True)
        nc.scalar.activation(floor[:], minus_cap[:], ACT.Sigmoid)

        hid_bf = keep.tile([P, Q, PACK], BF16, name="hid_bf", align_bytes=64)
        nc.scalar.copy(hid_bf[:], hid_raw[:].rearrange("p j q -> p q j"))
        last_cols = keep.tile([P, S_COLS], F32, name="last_cols", tag="hid_raw")
        load_weights(last_cols, s3)
        s_cols.append(last_cols)
        hid_words = keep.tile([P, Q], U32, name="hid_words", align_bytes=64)
        hid_scales = keep.tile([P, Q], U8, name="hid_scales", align_bytes=64)
        nc.vector.quantize_mx(
            out=hid_words[:].bitcast(FP8X4), scales=hid_scales[:], in_=hid_bf[:].rearrange("p q j -> p (q j)")
        )

        minus_s = []
        for k in range(TERMS):
            s_bank = psum.tile([P, S_COLS, P], F32, name="s_bank%d" % k)
            for c in range(S_COLS):
                nc.tensor.transpose(s_bank[:, c, :], s_cols[k][:, c : c + 1].to_broadcast([P, P]), ident[:])
            row = keep.tile([P, I], F32, name="minus_s%d" % k)
            nc.scalar.mul(row[:].rearrange("q (p c) -> q p c", c=S_COLS), s_bank[:].rearrange("q c p -> q p c"), -1.0)
            minus_s.append(row)

        for first, count in SCALE_PARTS:
            picked = keep.tile([P, count], U8, name="picked%d" % first, align_bytes=64)
            nc.vector.tensor_copy(picked[:], store_scales[:].indirect(entries(node_list, first, count)))
            rows = BLOCKS // QUADRANTS
            for quad in range(QUADRANTS):
                nc.sync.dma_start(
                    node_scales[QUADRANT_ROWS * quad : QUADRANT_ROWS * quad + rows, first : first + count].bitcast(I32),
                    picked[STAGED + rows * quad : STAGED + rows * (quad + 1), :].bitcast(I32),
                )

        scores = keep.tile([P, V], F32, name="scores")
        for first, passes in WORD_PARTS:
            count = sum(n for n, engine in passes)
            node_words = keep.tile([P, count], U32, name="node_words%d" % first, align_bytes=64)
            nc.vector.tensor_copy(node_words[:], store_words[:].indirect(entries(node_list, first, count)))
            at = 0
            for n, engine in passes:
                nodes = slice(first + at, first + at + n)
                score_bank = psum.tile([P, n], F32, name="score_bank%d" % nodes.start)
                nc.tensor.matmul_mx(
                    out=score_bank[:],
                    lhsT=hid_words[:].bitcast(FP8X4),
                    lhsT_scale=hid_scales[:],
                    rhs=node_words[:, at : at + n].bitcast(FP8X4),
                    rhs_scale=node_scales[:, nodes],
                    start=True,
                    stop=True,
                )
                copies[engine](scores[:, nodes], score_bank[:])
                at += n

        y = [keep.tile([P, I], F32, name="y%d" % k) for k in range(TERMS)]
        chance = [keep.tile([P, I], F32, name="chance%d" % k) for k in range(TERMS)]
        raised0 = keep.tile([P, I], F32, name="raised0")
        removed0 = keep.tile([P, I], F32, name="removed0")

        def look_up(k, first, count):
            cols = slice(first, first + count)
            picked_scores = scores[:].indirect(entries(path_lists[k], first, count))
            nc.vector.tensor_tensor(y[k][:, cols], picked_scores, minus_s[k][:, cols], ALU.mult)
            return cols

        for first, count in LOOKUP_PARTS[0]:
            cols = look_up(0, first, count)
            nc.scalar.activation(raised0[:, cols], y[0][:, cols], ACT.Relu, bias=plus_cap[:])
            nc.scalar.activation(chance[0][:, cols], raised0[:, cols], ACT.Sigmoid, bias=minus_cap[:])
        nc.scalar.activation(removed0[:], y[0][:], ACT.Relu, bias=minus_cap[:], scale=-1.0)
        for k in range(1, TERMS):
            for first, count in LOOKUP_PARTS[k]:
                cols = look_up(k, first, count)
                nc.scalar.activation(chance[k][:, cols], y[k][:, cols], ACT.Sigmoid)

        product01 = keep.tile([P, I], F32, name="product01")
        product = keep.tile([P, I], F32, name="product")
        below01 = keep.tile([P, I], F32, name="below01")
        below = keep.tile([P, I], F32, name="below")
        nc.vector.scalar_tensor_tensor(product01[:], chance[1][:], floor[:], chance[0][:], ALU.max, ALU.mult)
        nc.vector.scalar_tensor_tensor(below01[:], y[1][:], -CAP, removed0[:], ALU.min, ALU.subtract)
        nc.vector.scalar_tensor_tensor(product[:], chance[2][:], floor[:], product01[:], ALU.max, ALU.mult)
        nc.vector.scalar_tensor_tensor(below[:], y[2][:], -CAP, below01[:], ALU.min, ALU.add)

        result = keep.tile([P, I], F32, name="result")
        for first, count, queue in RESULT_PARTS:
            cols = slice(first, first + count)
            log_product = keep.tile([P, count], F32, name="log_product%d" % first)
            nc.scalar.activation(log_product[:], product[:, cols], ACT.Ln)
            nc.vector.scalar_tensor_tensor(result[:, cols], below[:, cols], 2 * CAP, log_product[:], ALU.add, ALU.add)
            queues[queue].dma_start(out[:, cols], result[:, cols])
